import numpy as np
import ml_dtypes


def mxq(x, axis, fmt="e4m3"):
    dtype, down = {"e4m3": (ml_dtypes.float8_e4m3fn, 7), "e5m2": (ml_dtypes.float8_e5m2, 14)}[fmt]
    v = np.moveaxis(np.asarray(x, np.float32).astype(ml_dtypes.bfloat16).astype(np.float64), axis, -1)
    blocks = v.reshape(v.shape[:-1] + (-1, 32))
    amax = np.abs(blocks).max(-1, keepdims=True)
    byte = np.maximum(np.where(amax > 0, np.frexp(amax)[1] - 1 + 127, 0) - down, 1)
    scale = np.exp2(byte - 127.0)
    codes = (blocks / scale).astype(np.float32).astype(dtype).astype(np.float64)
    return np.moveaxis((codes * scale).reshape(v.shape), -1, axis)


WIDE = False


def mx_kscale(k):
    if not WIDE:
        return np.ones(k)
    levels = np.array([10, -10, 5, -5, 0])
    if k % 512:
        return np.exp2(np.random.permutation(np.resize(levels, k // 32))).repeat(32)
    a = np.empty((k // 512, 16))
    for p in range(k // 512):
        a[p, :8] = np.random.permutation(np.resize(levels, 8))
        for g in range(8):
            far = levels[np.abs(levels - a[p, g]) >= 10]
            a[p, g + 8] = far[np.random.randint(len(far))]
    return np.exp2(a.ravel()).repeat(32)


def f64(x):
    return np.asarray(x).astype(np.float64)


def striped(idx):
    return np.tile(idx.reshape(-1, 16).T, (8, 1)).astype(np.uint16)


def unstriped(offs):
    return offs[:16].T.reshape(-1).astype(np.int64)


E2M1 = np.array([0.0, 0.5, 1.0, 1.5, 2.0, 3.0, 4.0, 6.0, -0.0, -0.5, -1.0, -1.5, -2.0, -3.0, -4.0, -6.0])


def pack_weight(w, fmt):
    k, n = w.shape
    w = f64(np.asarray(w, np.float32).astype(ml_dtypes.bfloat16)).reshape(k // 32, 32, n)
    amax = np.abs(w).max(1)
    if fmt == "e4m3":
        byte = np.frexp(amax)[1] - 1 + 127 - 7
    else:
        mant, ex = np.frexp(amax / 6.0)
        byte = np.where(mant > 0.5, ex, ex - 1) + 127
    byte = np.clip(np.where(amax > 0, byte, 1), 1, 254)
    scaled = (w * np.exp2(127.0 - byte)[:, None, :]).reshape(k, n).astype(np.float32)
    by_word = np.ascontiguousarray(scaled.reshape(k // 512, 128, 4, n).transpose(0, 1, 3, 2))
    if fmt == "e4m3":
        words = by_word.astype(ml_dtypes.float8_e4m3fn).view(np.uint8)
    else:
        c = by_word.astype(ml_dtypes.float4_e2m1fn).view(np.uint8) & 0xF
        words = (c[..., 0::2] | (c[..., 1::2] << 4)).reshape(k // 512, 128, 2 * n)
    return np.ascontiguousarray(words), np.ascontiguousarray(byte.astype(np.uint8).reshape(k // 512, 16, n))


def unpack_weight(words, scales, fmt):
    g, _, n = scales.shape
    words = np.ascontiguousarray(words).reshape(g, 128, n, -1)
    if fmt == "e4m3":
        vals = words.view(ml_dtypes.float8_e4m3fn).astype(np.float64)
    else:
        nib = np.empty((g, 128, n, 4), np.uint8)
        nib[..., 0::2] = words & 0xF
        nib[..., 1::2] = words >> 4
        vals = E2M1[nib]
    vals = vals * np.repeat(np.exp2(scales.astype(np.float64) - 127.0), 8, axis=1)[..., None]
    return vals.transpose(0, 1, 3, 2).reshape(g * 512, n)


def gelu(v):
    return 0.5 * v * (1.0 + np.tanh(np.sqrt(2.0 / np.pi) * (v + 0.044715 * v**3)))


K, T, S1, S2 = 512, 1024, 512, 512


def setup_inputs():
    n = np.random.standard_normal
    s = mx_kscale(K)
    u = mx_kscale(K)
    first, second = np.random.permutation(T)[:S1], np.random.permutation(T)[:S2]
    xf = n((K, T))
    x = pack_weight(xf * s[:, None], "e4m3")
    w1 = pack_weight(n((K, K)) / np.sqrt(K) / s[:, None] * u, "e2m1")
    w2 = pack_weight(n((K, K)) / np.sqrt(K) / u[:, None] * u, "e4m3")
    return {
        "x_words": x[0],
        "x_scales": x[1],
        "xr": (xf * u[:, None]).astype(np.float32),
        "w1_words": w1[0],
        "w1_scales": w1[1],
        "w2_words": w2[0],
        "w2_scales": w2[1],
        "gate1": (np.tile(np.random.uniform(0.2, 1.0, S1), (128, 1))).astype(np.float32),
        "gate2": (np.tile(np.random.uniform(0.2, 1.0, S2), (128, 1))).astype(np.float32),
        "offs": striped(first),
        "offs2": striped(second),
    }


def reference(x_words, x_scales, xr, w1_words, w1_scales, w2_words, w2_scales, gate1, gate2, offs, offs2):
    w1 = unpack_weight(w1_words, w1_scales, "e2m1")
    w2 = unpack_weight(w2_words, w2_scales, "e4m3")
    idx, idx2 = unstriped(offs), unstriped(offs2)
    r = f64(xr)
    r[:, idx] += f64(gate1[:1]) * gelu(w1.T @ unpack_weight(x_words, x_scales, "e4m3")[:, idx])
    r2 = r.copy()
    r2[:, idx2] += f64(gate2[:1]) * gelu(w2.T @ mxq(r[:, idx2], 0, "e4m3"))
    return r2

from contextlib import ExitStack

import concourse.mybir as mybir
from concourse.masks import make_identity

K, T, S = 512, 1024, 512
FLOPS = 2 * 2 * K * K * S

F32 = mybir.dt.float32
BF16 = mybir.dt.bfloat16
I32 = mybir.dt.int32
U32 = mybir.dt.uint32
U16 = mybir.dt.uint16
U8 = mybir.dt.uint8
FP8X4 = mybir.dt.float8_e4m3fn_x4
FP4X4 = mybir.dt.float4_e2m1fn_x4
GELU = mybir.ActivationFunctionType.Gelu_apprx_tanh
COPY = mybir.ActivationFunctionType.Copy
MULT = mybir.AluOpType.mult
ADD = mybir.AluOpType.add

P = 128
PACK = 4
HALF = S // 2
LEAD = 128
BANK = 512


def tile_moe_mod_gelu_kernel(
    tc, x_words, x_scales, xr, w1_words, w1_scales, w2_words, w2_scales, gate1, gate2, offs, offs2, out
):
    nc = tc.nc
    with ExitStack() as ctx:
        keep = ctx.enter_context(tc.tile_pool(name="keep", bufs=1))
        stage = ctx.enter_context(tc.tile_pool(name="stage", bufs=2))
        shared = ctx.enter_context(tc.tile_pool(name="shared", bufs=1))
        psum = ctx.enter_context(tc.psum_pool(name="psum", bufs=2))

        def sb(name, cols, dtype):
            return keep.tile([P, cols], dtype, name=name, align_bytes=64)

        list1 = keep.tile([P, S // 16], U16, name="list1")
        list2 = keep.tile([P, S // 16], U16, name="list2")
        xw = sb("xw", T, U32)
        xs = sb("xs", T, U8)
        xw_g = sb("xw_g", S, U32)
        xs_g = sb("xs_g", S, U8)
        w1_raw = sb("w1_raw", 2 * K, U8)
        w1s_raw = sb("w1s_raw", K, U8)
        w1 = sb("w1", 2 * K, U8)
        w1s = sb("w1s", K, U8)
        w2_raw = sb("w2_raw", K, I32)
        w2s_raw = sb("w2s_raw", K, U8)
        w2 = sb("w2", K, I32)
        w2s = sb("w2s", K, U8)
        g1 = sb("g1", S, F32)
        g2 = sb("g2", S, F32)
        res = [sb("res%d" % t, T, F32) for t in range(PACK)]
        add1 = [sb("add1_%d" % t, T, F32) for t in range(PACK)]
        add2 = [sb("add2_%d" % t, T, F32) for t in range(PACK)]
        y = [sb("y%d" % t, S, F32) for t in range(PACK)]
        z = [sb("z%d" % t, S, F32) for t in range(PACK)]
        r16 = [None, sb("r16_1", T, BF16), None, sb("r16_3", T, BF16)]
        grouped = [
            keep.tile([P, PACK * LEAD], BF16, name="grouped0", tag="reused", align_bytes=64),
            sb("grouped1", PACK * (S - LEAD), BF16),
        ]
        r_codes = sb("r_codes", S, U32)
        r_scales = sb("r_scales", S, U8)
        ident32 = sb("ident32", P, F32)
        ident16 = sb("ident16", P, BF16)
        warm = sb("warm", 16, F32)
        last = PACK - 1
        whole, front, rear = slice(0, S), slice(0, HALF), slice(HALF, S)
        lead, rest = slice(0, LEAD), slice(LEAD, S)

        def load_scales(plane, rows):
            for q in range(4):
                nc.sync.dma_start(out=plane[32 * q : 32 * q + 4, :].bitcast(I32), in_=rows[4 * q : 4 * q + 4, :].bitcast(I32))

        def entries(lst, n):
            return lst[:, n.start // 16 : n.stop // 16]

        def permute(dst, src, t0, t1):
            nc.vector.tensor_copy(
                out=dst.rearrange("p (t m) -> p t m", t=PACK)[:, t0:t1, :],
                in_=src.rearrange("p (m t) -> p t m", t=PACK)[:, t0:t1, :],
            )

        for plane in (w1s_raw, xs, w2s_raw):
            nc.gpsimd.memset(plane[:].bitcast(I32), 0)
        nc.vector.memset(add2[last][:].bitcast(I32), 0)
        nc.vector.memset(add1[0][:].bitcast(I32), 0)
        nc.scalar.activation(warm[:], add2[last][:, 0:16], GELU)
        for t in range(1, PACK):
            nc.scalar.copy(add1[t][:], add2[last][:])
        make_identity(nc, ident32[:])
        make_identity(nc, ident16[:])

        xr_rows = xr.rearrange("(p t) n -> p t n", t=PACK)
        out_rows = out.rearrange("(p t) n -> p t n", t=PACK)
        nc.sync.dma_start(list1[:], offs)
        load_scales(w1s_raw, w1_scales[0])
        nc.sync.dma_start(out=w1_raw[:].bitcast(I32), in_=w1_words[0].bitcast(I32))
        nc.sync.dma_start(out=xw[:].bitcast(I32), in_=x_words[0].rearrange("p n d -> p (n d)").bitcast(I32))
        load_scales(xs, x_scales[0])
        nc.sync.dma_start(out=g1[:], in_=gate1)
        nc.sync.dma_start(list2[:], offs2)
        for t in range(PACK):
            nc.sync.dma_start(out=res[t][:], in_=xr_rows[:, t, :])
        nc.sync.dma_start(out=w2_raw[:], in_=w2_words[0].rearrange("p n d -> p (n d)").bitcast(I32))
        load_scales(w2s_raw, w2_scales[0])
        nc.sync.dma_start(out=g2[:], in_=gate2)
        for t in range(last):
            nc.sync.dma_start(out=add2[t][:], in_=add2[last][:])

        def gather_words(n):
            nc.vector.tensor_copy(xw_g[:, n], xw[:].indirect(entries(list1, n)))

        def gather_scales(n):
            nc.vector.tensor_copy(xs_g[:, n], xs[:].indirect(entries(list1, n)))

        def layer1(t, n, dst):
            acc = psum.tile([P, BANK], F32, name="acc", tag="acc", bufs=2)
            nc.tensor.matmul_mx(
                out=acc[:, n],
                lhsT=w1[:, 2 * P * t : 2 * P * (t + 1)].bitcast(FP4X4),
                lhsT_scale=w1s[:, P * t : P * (t + 1)],
                rhs=xw_g[:, n].bitcast(FP8X4),
                rhs_scale=xs_g[:, n],
                start=True,
                stop=True,
            )
            nc.scalar.activation(dst, acc[:, n], GELU)

        def layer2(t, parts):
            acc = psum.tile([P, BANK], F32, name="acc", tag="acc", bufs=2)
            for n in parts:
                nc.tensor.matmul_mx(
                    out=acc[:, n],
                    lhsT=w2[:, P * t : P * (t + 1)].bitcast(FP8X4),
                    lhsT_scale=w2s[:, P * t : P * (t + 1)],
                    rhs=r_codes[:, n].bitcast(FP8X4),
                    rhs_scale=r_scales[:, n],
                    start=True,
                    stop=True,
                )
            n = slice(parts[0].start, parts[-1].stop)
            nc.scalar.activation(z[t][:, n], acc[:, n], GELU)

        def scatter(window, lst, values, gate, n):
            nc.vector.tensor_tensor(window[:].indirect(entries(lst, n)), values, gate[:, n], MULT)

        def turn_in(banks, src, first, final):
            for b in range(2):
                for c in range(4):
                    col = BANK * b + P * c
                    nc.tensor.matmul(
                        banks[b][:, P * c : P * (c + 1)],
                        lhsT=src[:, col : col + P],
                        rhs=ident32[:],
                        start=(first and c == 0),
                        stop=(final and c == 3),
                        is_transpose=True,
                    )

        def new_banks(tag, dtype, bufs=1):
            if bufs == 1:
                return [psum.tile([P, BANK], dtype, name="pair", tag="%s%d" % (tag, b), bufs=1) for b in range(2)]
            return [psum.tile([P, BANK], dtype, name="pair", tag=tag, bufs=bufs) for b in range(2)]

        def leave(banks, turned):
            for b in range(2):
                nc.scalar.copy(turned[:, BANK * b : BANK * (b + 1)], banks[b][:])

        def turn_back(turned, banks, ident, dst):
            for b in range(2):
                for c in range(4):
                    col = BANK * b + P * c
                    nc.tensor.transpose(banks[b][:, P * c : P * (c + 1)], turned[:, col : col + P], ident[:])
                nc.scalar.copy(dst[:, BANK * b : BANK * (b + 1)], banks[b][:])

        def gather_r(t, h):
            dst = grouped[h][:].rearrange("p (m t) -> p m t", t=PACK)[:, :, t]
            nc.scalar.activation(dst, r16[t][:].indirect(entries(list2, (lead, rest)[h])), COPY)

        def quantize(h, n):
            first = (lead, rest)[h].start
            values = grouped[h][:, PACK * (n.start - first) : PACK * (n.stop - first)]
            nc.vector.quantize_mx(out=r_codes[:, n].bitcast(FP8X4), scales=r_scales[:, n], in_=values)

        permute(w1s[:], w1s_raw[:], 0, PACK)
        permute(w1[:].bitcast(U16), w1_raw[:].bitcast(U16), 0, PACK)
        gather_words(front)
        gather_scales(front)
        layer1(0, front, y[0][:, front])
        gather_words(rear)
        gather_scales(rear)
        layer1(0, rear, y[0][:, rear])
        layer1(1, whole, y[1][:])
        layer1(2, whole, y[2][:])
        layer1(last, front, y[last][:, front])
        scatter(add1[0], list1, y[0][:, front], g1, front)
        scatter(add1[0], list1, y[0][:, rear], g1, rear)
        scatter(add1[1], list1, y[1][:], g1, whole)
        scatter(add1[2], list1, y[2][:], g1, whole)

        sums = new_banks("x", F32)
        turn_in(sums, res[0], True, False)
        turn_in(sums, add1[0], False, True)
        turned = sb("turned0", T, BF16)
        leave(sums, turned)
        r16[0] = shared.tile([P, T], BF16, name="r16_0", offset=1024, align_bytes=64)
        turn_back(turned, new_banks("y", BF16), ident16, r16[0])
        gather_r(0, 0)
        gather_r(0, 1)

        sums = new_banks("y", F32)
        turn_in(sums, res[1], True, False)
        turn_in(sums, add1[1], False, True)
        turned = shared.tile([P, T], BF16, name="turned1", offset=1024, align_bytes=64)
        leave(sums, turned)
        turn_back(turned, new_banks("z", BF16), ident16, r16[1])
        y_end = shared.tile([P, HALF], F32, name="y_end", offset=2048, align_bytes=64)
        layer1(last, rear, y_end[:])
        gather_r(1, 0)
        gather_r(1, 1)

        r16[2] = shared.tile([P, T], BF16, name="r16_2", offset=0, align_bytes=64)
        nc.vector.tensor_tensor(r16[2][:], res[2][:], add1[2][:], ADD)
        scatter(add1[last], list1, y[last][:, front], g1, front)
        scatter(add1[last], list1, y_end[:], g1, rear)
        nc.vector.tensor_tensor(r16[last][:], res[last][:], add1[last][:], ADD)
        permute(w2[:], w2_raw[:], 0, PACK)
        permute(w2s[:], w2s_raw[:], 0, PACK)
        gather_r(2, 0)
        gather_r(2, 1)
        gather_r(last, 0)

        middle = slice(LEAD, HALF)
        quantize(0, lead)
        layer2(0, [lead])
        r_last = keep.tile([P, T], F32, name="r_last", tag="reused", align_bytes=64)
        nc.vector.tensor_tensor(r_last[:], res[last][:], add1[last][:], ADD)
        gather_r(last, 1)
        layer2(1, [lead])
        scatter(add2[0], list2, z[0][:, lead], g2, lead)
        quantize(1, middle)
        quantize(1, rear)
        layer2(0, [middle, rear])
        layer2(1, [middle, rear])
        layer2(2, [whole])
        layer2(last, [whole])
        scatter(add2[1], list2, z[1][:, lead], g2, lead)
        scatter(add2[0], list2, z[0][:, rest], g2, rest)
        scatter(add2[1], list2, z[1][:, rest], g2, rest)
        scatter(add2[2], list2, z[2][:], g2, whole)
        scatter(add2[last], list2, z[last][:], g2, whole)
        totals = [new_banks("y", F32), new_banks("z", F32), new_banks("acc", F32, 2)]
        for t in range(last):
            turn_in(totals[t], res[t], True, False)
            turn_in(totals[t], add1[t], False, False)

        for t in range(last):
            turn_in(totals[t], add2[t], False, True)
            turned = stage.tile([P, T], F32, name="turned", tag="turned", bufs=3)
            leave(totals[t], turned)
            done = stage.tile([P, T], F32, name="done", tag="done", bufs=4)
            turn_back(turned, new_banks("xyz"[t], F32), ident32, done)
            for b in range(2):
                nc.sync.dma_start(out=out_rows[:, t, BANK * b : BANK * (b + 1)], in_=done[:, BANK * b : BANK * (b + 1)])
        done = stage.tile([P, T], F32, name="done", tag="done", bufs=4)
        for b in range(2):
            cols = slice(BANK * b, BANK * (b + 1))
            nc.vector.tensor_tensor(done[:, cols], r_last[:, cols], add2[last][:, cols], ADD)
            nc.sync.dma_start(out=out_rows[:, last, cols], in_=done[:, cols])
